import numpy as np
import ml_dtypes


def mxq(x, axis, fmt="e4m3"):
    dtype, down = {"e4m3": (ml_dtypes.float8_e4m3fn, 7), "e5m2": (ml_dtypes.float8_e5m2, 14)}[fmt]
    v = np.moveaxis(np.asarray(x, np.float32).astype(ml_dtypes.bfloat16).astype(np.float64), axis, -1)
    blocks = v.reshape(v.shape[:-1] + (-1, 32))
    amax = np.abs(blocks).max(-1, keepdims=True)
    byte = np.maximum(np.where(amax > 0, np.frexp(amax)[1] - 1 + 127, 0) - down, 1)
    scale = np.exp2(byte - 127.0)
    codes = (blocks / scale).astype(np.float32).astype(dtype).astype(np.float64)
    return np.moveaxis((codes * scale).reshape(v.shape), -1, axis)


WIDE = False


def mx_kscale(k):
    if not WIDE:
        return np.ones(k)
    levels = np.array([10, -10, 5, -5, 0])
    if k % 512:
        return np.exp2(np.random.permutation(np.resize(levels, k // 32))).repeat(32)
    a = np.empty((k // 512, 16))
    for p in range(k // 512):
        a[p, :8] = np.random.permutation(np.resize(levels, 8))
        for g in range(8):
            far = levels[np.abs(levels - a[p, g]) >= 10]
            a[p, g + 8] = far[np.random.randint(len(far))]
    return np.exp2(a.ravel()).repeat(32)


def f64(x):
    return np.asarray(x).astype(np.float64)


def striped(idx):
    return np.tile(idx.reshape(-1, 16).T, (8, 1)).astype(np.uint16)


def unstriped(offs):
    return offs[:16].T.reshape(-1).astype(np.int64)


def pack_weight(w):
    k, n = w.shape
    w = f64(np.asarray(w, np.float32).astype(ml_dtypes.bfloat16)).reshape(k // 32, 32, n)
    amax = np.abs(w).max(1)
    byte = np.clip(np.where(amax > 0, np.frexp(amax)[1] - 1 + 127 - 7, 1), 1, 254)
    scaled = (w * np.exp2(127.0 - byte)[:, None, :]).reshape(k, n).astype(np.float32)
    words = np.ascontiguousarray(scaled.reshape(k // 512, 128, 4, n).transpose(0, 1, 3, 2)).astype(ml_dtypes.float8_e4m3fn).view(np.uint8)
    return words, np.ascontiguousarray(byte.astype(np.uint8).reshape(k // 512, 16, n))


def unpack_weight(words, scales):
    g, p, n, _ = words.shape
    vals = np.ascontiguousarray(words).view(ml_dtypes.float8_e4m3fn).astype(np.float64) * np.repeat(np.exp2(scales.astype(np.float64) - 127.0), 8, axis=1)[..., None]
    return vals.transpose(0, 1, 3, 2).reshape(g * 512, n)


K, T, S, V, H, N = 1024, 1024, 768, 256, 512, 128


def setup_inputs():
    n = np.random.standard_normal
    s = mx_kscale(K)[:, None]
    u = mx_kscale(H)
    packed_w4 = pack_weight(n((H, N)) / np.sqrt(H) / u[:, None])
    return {
        "xT": (n((K, T)) * s).astype(np.float32),
        "w1": (n((K, H)) / np.sqrt(K) / s * u).astype(np.float32),
        "w2": (n((K, H)) / np.sqrt(K) / s).astype(np.float32),
        "w3": (n((K, H)) / np.sqrt(K) / s).astype(np.float32),
        "w4_words": packed_w4[0],
        "w4_scales": packed_w4[1],
        "offs": striped(np.random.permutation(T)[:S]),
    }


def reference(xT, w1, w2, w3, w4_words, w4_scales, offs):
    xq = mxq(f64(xT)[:, unstriped(offs)], 0, "e4m3")
    z = (((mxq(f64(w1), 0, "e4m3").T @ xq[:, :V])) * ((mxq(f64(w2), 0, "e4m3").T @ xq[:, V:2 * V]))) * ((mxq(f64(w3), 0, "e4m3").T @ xq[:, 2 * V:3 * V]))
    return unpack_weight(w4_words, w4_scales).T @ mxq(z, 0, "e4m3")

@@ -1,0 +1,212 @@
+from contextlib import ExitStack
+
+import concourse.mybir as mybir
+
+K, T, S, V, H, N = 1024, 1024, 768, 256, 512, 128
+FLOPS = 3 * 2 * K * H * V + 2 * H * N * V
+
+F32 = mybir.dt.float32
+BF16 = mybir.dt.bfloat16
+I32 = mybir.dt.int32
+U32 = mybir.dt.uint32
+U16 = mybir.dt.uint16
+U8 = mybir.dt.uint8
+FP8X4 = mybir.dt.float8_e4m3fn_x4
+MULT = mybir.AluOpType.mult
+
+P = 128
+PACK = 4
+K_PASS = P * PACK
+X_COLS = 512
+HALF = V // 2
+
+
+def tile_picked_trilin_none_e_kernel(
+    tc, xT, w1, w2, w3, w4_words, w4_scales, offs, out
+):
+    nc = tc.nc
+    with ExitStack() as ctx:
+        keep = ctx.enter_context(tc.tile_pool(name="keep", bufs=1))
+        psum = ctx.enter_context(tc.psum_pool(name="psum", bufs=1))
+
+        def rows_of(src, g, c0, c1, name):
+            raw = keep.tile([P, PACK, c1 - c0], F32, name=name)
+            rows = src[g * K_PASS : (g + 1) * K_PASS, c0:c1]
+            nc.sync.dma_start(out=raw[:], in_=rows.rearrange("(p j) w -> p j w", j=PACK))
+            return raw
+
+        x_scales = keep.tile([P, T], U8, name="x_scales", align_bytes=64)
+        nc.gpsimd.memset(x_scales[:], 0)
+        w4_plane = keep.tile([P, N], U8, name="w4_plane", align_bytes=64)
+        nc.vector.memset(w4_plane[:].bitcast(I32), 0)
+        offsets = keep.tile([P, S // 16], U16, name="offsets")
+
+        x_raw = {}
+        x_raw[0, 0] = rows_of(xT, 0, 0, X_COLS, "x_raw00")
+        nc.sync.dma_start(offsets[:], offs)
+        x_raw[0, 1] = rows_of(xT, 0, X_COLS, T, "x_raw01")
+        for q in range(4):
+            nc.scalar.dma_start(
+                out=w4_plane[32 * q : 32 * q + 4, :].bitcast(I32),
+                in_=w4_scales[0, 4 * q : 4 * q + 4, :].bitcast(I32),
+            )
+        x_raw[1, 0] = rows_of(xT, 1, 0, X_COLS, "x_raw10")
+        x_raw[1, 1] = rows_of(xT, 1, X_COLS, T, "x_raw11")
+        w_raw = {}
+        for d, w in enumerate((w1, w2, w3)):
+            for g in range(2):
+                if (d, g) != (2, 1):
+                    w_raw[d, g] = rows_of(w, g, 0, H, "w_raw%d%d" % (d, g))
+        w4_codes = keep.tile([P, N], U32, name="w4_codes", align_bytes=64)
+        nc.sync.dma_start(
+            out=w4_codes[:].bitcast(I32),
+            in_=w4_words[0].rearrange("p n t -> p (n t)").bitcast(I32),
+        )
+        last_raw = [rows_of(w3, 1, u * (H // 2), (u + 1) * (H // 2), "last_raw%d" % u) for u in range(2)]
+
+        x_codes = [keep.tile([P, T], U32, name="x_codes%d" % g, align_bytes=64) for g in range(2)]
+        got_codes = [keep.tile([P, S], U32, name="got_codes%d" % g, align_bytes=64) for g in range(2)]
+        got_scales = keep.tile([P, S], U8, name="got_scales", align_bytes=64)
+
+        def round_x(g, u, on_vector):
+            raw = x_raw[g, u]
+            grouped = keep.tile([P, X_COLS, PACK], BF16, name="x_bf%d%d" % (g, u), align_bytes=64)
+            for copy, c0, c1 in ((nc.scalar.copy, on_vector, X_COLS), (nc.vector.tensor_copy, 0, on_vector)):
+                if c1 > c0:
+                    copy(
+                        grouped[:, c0:c1, :].rearrange("p (c i) j -> p c j i", i=4),
+                        raw[:, :, c0:c1].rearrange("p j (c i) -> p c j i", i=4),
+                    )
+            return grouped
+
+        def quantise_x(g, u, grouped):
+            cols = slice(u * X_COLS, (u + 1) * X_COLS)
+            nc.vector.quantize_mx(
+                out=x_codes[g][:, cols].bitcast(FP8X4),
+                scales=x_scales[4 * g : P, cols],
+                in_=grouped[:].rearrange("p c j -> p (c j)"),
+            )
+
+        def round_w(d, g, on_vector):
+            raw = w_raw[d, g]
+            grouped = keep.tile([P, PACK, P, PACK], BF16, name="w_bf%d%d" % (d, g), align_bytes=64)
+            for copy, m0, m1 in ((nc.scalar.copy, on_vector, P), (nc.vector.tensor_copy, 0, on_vector)):
+                if m1 > m0:
+                    copy(
+                        grouped[:, :, m0:m1, :].rearrange("p t m j -> p m j t"),
+                        raw[:, :, 4 * m0 : 4 * m1].rearrange("p j (m t) -> p m j t", t=4),
+                    )
+            return grouped
+
+        w_codes = {}
+        w_scales = {}
+        for d in range(3):
+            for g in range(2):
+                w_codes[d, g] = keep.tile([P, H], U32, name="w_codes%d%d" % (d, g), align_bytes=64)
+                w_scales[d, g] = keep.tile([P, H], U8, name="w_scales%d%d" % (d, g), align_bytes=64)
+
+        def quantise_w(d, g, grouped, calls):
+            flat = grouped[:].rearrange("p t m j -> p (t m j)")
+            width = H // calls
+            for c in range(calls):
+                cols = slice(c * width, (c + 1) * width)
+                nc.vector.quantize_mx(
+                    out=w_codes[d, g][:, cols].bitcast(FP8X4),
+                    scales=w_scales[d, g][:, cols],
+                    in_=flat[:, PACK * c * width : PACK * (c + 1) * width],
+                )
+
+        def product_pass(d, g, banks):
+            piece = slice(d * V, (d + 1) * V)
+            for t in range(PACK):
+                cols = slice(t * P, (t + 1) * P)
+                nc.tensor.matmul_mx(
+                    out=banks[t][:],
+                    lhsT=w_codes[d, g][:, cols].bitcast(FP8X4),
+                    lhsT_scale=w_scales[d, g][:, cols],
+                    rhs=got_codes[g][:, piece].bitcast(FP8X4),
+                    rhs_scale=got_scales[4 * g : P, piece],
+                    start=(g == 0),
+                    stop=(g == 1),
+                )
+
+        quantise_x(0, 0, round_x(0, 0, 320))
+        quantise_x(0, 1, round_x(0, 1, 224))
+        nc.vector.tensor_copy(got_codes[0][:], x_codes[0][:].indirect(offsets[:]))
+        quantise_x(1, 0, round_x(1, 0, 64))
+        quantise_x(1, 1, round_x(1, 1, 288))
+        nc.vector.tensor_copy(got_codes[1][:], x_codes[1][:].indirect(offsets[:]))
+        nc.vector.tensor_copy(got_scales[:], x_scales[:].indirect(offsets[:]))
+
+        banks_a = [psum.tile([P, V], F32, name="a%d" % t, tag="low%d" % t) for t in range(PACK)]
+        quantise_w(0, 0, round_w(0, 0, 0), 1)
+        product_pass(0, 0, banks_a)
+        quantise_w(0, 1, round_w(0, 1, 40), 2)
+        product_pass(0, 1, banks_a)
+
+        banks_b = [psum.tile([P, V], F32, name="b%d" % t, tag="high%d" % t) for t in range(PACK)]
+        quantise_w(1, 0, round_w(1, 0, 56), 1)
+        product_pass(1, 0, banks_b)
+        a_sb = keep.tile([P, PACK, V], F32, name="a_sb")
+        for t in range(PACK):
+            nc.scalar.copy(a_sb[:, t, :], banks_a[t][:])
+        quantise_w(1, 1, round_w(1, 1, 80), 4)
+        product_pass(1, 1, banks_b)
+        ab = keep.tile([P, PACK, V], F32, name="ab")
+        for t in range(PACK):
+            nc.vector.tensor_tensor(ab[:, t, :], banks_b[t][:], a_sb[:, t, :], MULT)
+
+        banks_c = [psum.tile([P, V], F32, name="c%d" % t, tag="low%d" % t) for t in range(PACK)]
+        quantise_w(2, 0, round_w(2, 0, 40), 1)
+        product_pass(2, 0, banks_c)
+
+        for u in range(2):
+            grouped = keep.tile([P, PACK, P // 2, PACK], BF16, name="last_bf%d" % u, align_bytes=64)
+            by_t = last_raw[u][:].rearrange("p j (m t) -> p m j t", t=4)
+            nc.scalar.copy(grouped[:, 2:4, :, :].rearrange("p t m j -> p m j t"), by_t[:, :, :, 2:4])
+            nc.vector.tensor_copy(grouped[:, 0:2, :, :].rearrange("p t m j -> p m j t"), by_t[:, :, :, 0:2])
+            for t in range(PACK):
+                cols = slice(t * P + u * 64, t * P + (u + 1) * 64)
+                nc.vector.quantize_mx(
+                    out=w_codes[2, 1][:, cols].bitcast(FP8X4),
+                    scales=w_scales[2, 1][:, cols],
+                    in_=grouped[:, t, :, :].rearrange("p m j -> p (m j)"),
+                )
+        product_pass(2, 1, banks_c)
+
+        z_rows = keep.tile([P, PACK, V], BF16, name="z_rows", align_bytes=64)
+        for t in range(PACK - 1):
+            nc.vector.tensor_tensor(z_rows[:, t, :], banks_c[t][:], ab[:, t, :], MULT)
+        t = PACK - 1
+        for h in range(2):
+            cols = slice(h * HALF, (h + 1) * HALF)
+            nc.vector.tensor_tensor(z_rows[:, t, cols], banks_c[t][:, cols], ab[:, t, cols], MULT)
+        z_grouped = []
+        for h, copy in enumerate((nc.scalar.copy, nc.vector.tensor_copy)):
+            grouped = keep.tile([P, HALF, PACK], BF16, name="z_bf%d" % h, align_bytes=64)
+            copy(
+                grouped[:].rearrange("p (c i) t -> p c t i", i=4),
+                z_rows[:, :, h * HALF : (h + 1) * HALF].rearrange("p t (c i) -> p c t i", i=4),
+            )
+            z_grouped.append(grouped)
+        for h, copy in enumerate((nc.scalar.copy, nc.vector.tensor_copy)):
+            z_codes = keep.tile([P, HALF], U32, name="z_codes%d" % h, align_bytes=64)
+            z_scales = keep.tile([P, HALF], U8, name="z_scales%d" % h, align_bytes=64)
+            nc.vector.quantize_mx(
+                out=z_codes[:].bitcast(FP8X4),
+                scales=z_scales[:],
+                in_=z_grouped[h][:].rearrange("p c t -> p (c t)"),
+            )
+            acc = psum.tile([P, HALF], F32, name="acc%d" % h, tag="high%d" % h)
+            nc.tensor.matmul_mx(
+                out=acc[:],
+                lhsT=w4_codes[:].bitcast(FP8X4),
+                lhsT_scale=w4_plane[:],
+                rhs=z_codes[:].bitcast(FP8X4),
+                rhs_scale=z_scales[:],
+                start=True,
+                stop=True,
+            )
+            result = keep.tile([P, HALF], F32, name="result%d" % h)
+            copy(result[:], acc[:])
+            nc.sync.dma_start(out=out[:, h * HALF : (h + 1) * HALF], in_=result[:])

@@ -19,6 +19,7 @@ PACK = 4
 K_PASS = P * PACK
 X_COLS = 512
 HALF = V // 2
+X_PIECES = {(0, 0): slice(0, 512), (0, 1): slice(512, 1024), (1, 0): slice(0, 512), (1, 1): slice(512, 768), (1, 2): slice(768, 1024)}
 
 
 def tile_picked_trilin_none_e_kernel(
@@ -51,18 +52,19 @@ def tile_picked_trilin_none_e_kernel(
                 in_=w4_scales[0, 4 * q : 4 * q + 4, :].bitcast(I32),
             )
         x_raw[1, 0] = rows_of(xT, 1, 0, X_COLS, "x_raw10")
-        x_raw[1, 1] = rows_of(xT, 1, X_COLS, T, "x_raw11")
+        x_raw[1, 1] = rows_of(xT, 1, X_COLS, 768, "x_raw11")
+        x_raw[1, 2] = rows_of(xT, 1, 768, T, "x_raw12")
         w_raw = {}
         for d, w in enumerate((w1, w2, w3)):
             for g in range(2):
                 if (d, g) != (2, 1):
                     w_raw[d, g] = rows_of(w, g, 0, H, "w_raw%d%d" % (d, g))
+        last_raw = [rows_of(w3, 1, u * (H // 2), (u + 1) * (H // 2), "last_raw%d" % u) for u in range(2)]
         w4_codes = keep.tile([P, N], U32, name="w4_codes", align_bytes=64)
         nc.sync.dma_start(
             out=w4_codes[:].bitcast(I32),
             in_=w4_words[0].rearrange("p n t -> p (n t)").bitcast(I32),
         )
-        last_raw = [rows_of(w3, 1, u * (H // 2), (u + 1) * (H // 2), "last_raw%d" % u) for u in range(2)]
 
         x_codes = [keep.tile([P, T], U32, name="x_codes%d" % g, align_bytes=64) for g in range(2)]
         got_codes = [keep.tile([P, S], U32, name="got_codes%d" % g, align_bytes=64) for g in range(2)]
@@ -70,8 +72,9 @@ def tile_picked_trilin_none_e_kernel(
 
         def round_x(g, u, on_vector):
             raw = x_raw[g, u]
-            grouped = keep.tile([P, X_COLS, PACK], BF16, name="x_bf%d%d" % (g, u), align_bytes=64)
-            for copy, c0, c1 in ((nc.scalar.copy, on_vector, X_COLS), (nc.vector.tensor_copy, 0, on_vector)):
+            width = raw.shape[2]
+            grouped = keep.tile([P, width, PACK], BF16, name="x_bf%d%d" % (g, u), align_bytes=64)
+            for copy, c0, c1 in ((nc.scalar.copy, on_vector, width), (nc.vector.tensor_copy, 0, on_vector)):
                 if c1 > c0:
                     copy(
                         grouped[:, c0:c1, :].rearrange("p (c i) j -> p c j i", i=4),
@@ -80,7 +83,7 @@ def tile_picked_trilin_none_e_kernel(
             return grouped
 
         def quantise_x(g, u, grouped):
-            cols = slice(u * X_COLS, (u + 1) * X_COLS)
+            cols = X_PIECES[g, u]
             nc.vector.quantize_mx(
                 out=x_codes[g][:, cols].bitcast(FP8X4),
                 scales=x_scales[4 * g : P, cols],
@@ -116,78 +119,86 @@ def tile_picked_trilin_none_e_kernel(
                     in_=flat[:, PACK * c * width : PACK * (c + 1) * width],
                 )
 
-        def product_pass(d, g, banks):
-            piece = slice(d * V, (d + 1) * V)
-            for t in range(PACK):
-                cols = slice(t * P, (t + 1) * P)
-                nc.tensor.matmul_mx(
-                    out=banks[t][:],
-                    lhsT=w_codes[d, g][:, cols].bitcast(FP8X4),
-                    lhsT_scale=w_scales[d, g][:, cols],
-                    rhs=got_codes[g][:, piece].bitcast(FP8X4),
-                    rhs_scale=got_scales[4 * g : P, piece],
-                    start=(g == 0),
-                    stop=(g == 1),
-                )
+        def one_pass(d, g, t, h, bank):
+            cols = slice(t * P, (t + 1) * P)
+            picked = slice(d * V + h * HALF, d * V + (h + 1) * HALF)
+            nc.tensor.matmul_mx(
+                out=bank[:, t, :],
+                lhsT=w_codes[d, g][:, cols].bitcast(FP8X4),
+                lhsT_scale=w_scales[d, g][:, cols],
+                rhs=got_codes[g][:, picked].bitcast(FP8X4),
+                rhs_scale=got_scales[4 * g : P, picked],
+                start=(g == 0),
+                stop=(g == 1),
+            )
 
-        quantise_x(0, 0, round_x(0, 0, 320))
-        quantise_x(0, 1, round_x(0, 1, 224))
+        def open_product(d):
+            banks = [psum.tile([P, PACK, HALF], F32, name="sum%d%d" % (d, h)) for h in range(2)]
+            for h in range(2):
+                one_pass(d, 0, 0, h, banks[h])
+            return banks
+
+        def close_product(d, banks):
+            for h in range(2):
+                one_pass(d, 1, 0, h, banks[h])
+                for t in range(1, PACK):
+                    one_pass(d, 0, t, h, banks[h])
+                    one_pass(d, 1, t, h, banks[h])
+
+        def by_triple(bank):
+            return bank[:].rearrange("p t v -> p v t")
+
+        quantise_x(0, 0, round_x(0, 0, 384))
+        quantise_x(0, 1, round_x(0, 1, 320))
         nc.vector.tensor_copy(got_codes[0][:], x_codes[0][:].indirect(offsets[:]))
-        quantise_x(1, 0, round_x(1, 0, 64))
-        quantise_x(1, 1, round_x(1, 1, 288))
+        quantise_x(1, 0, round_x(1, 0, 128))
+        quantise_x(1, 1, round_x(1, 1, 160))
+        quantise_x(1, 2, round_x(1, 2, 64))
         nc.vector.tensor_copy(got_codes[1][:], x_codes[1][:].indirect(offsets[:]))
         nc.vector.tensor_copy(got_scales[:], x_scales[:].indirect(offsets[:]))
 
-        banks_a = [psum.tile([P, V], F32, name="a%d" % t, tag="low%d" % t) for t in range(PACK)]
         quantise_w(0, 0, round_w(0, 0, 0), 1)
-        product_pass(0, 0, banks_a)
-        quantise_w(0, 1, round_w(0, 1, 40), 2)
-        product_pass(0, 1, banks_a)
+        banks_a = open_product(0)
+        quantise_w(0, 1, round_w(0, 1, 48), 1)
+        close_product(0, banks_a)
 
-        banks_b = [psum.tile([P, V], F32, name="b%d" % t, tag="high%d" % t) for t in range(PACK)]
-        quantise_w(1, 0, round_w(1, 0, 56), 1)
-        product_pass(1, 0, banks_b)
-        a_sb = keep.tile([P, PACK, V], F32, name="a_sb")
-        for t in range(PACK):
-            nc.scalar.copy(a_sb[:, t, :], banks_a[t][:])
-        quantise_w(1, 1, round_w(1, 1, 80), 4)
-        product_pass(1, 1, banks_b)
-        ab = keep.tile([P, PACK, V], F32, name="ab")
-        for t in range(PACK):
-            nc.vector.tensor_tensor(ab[:, t, :], banks_b[t][:], a_sb[:, t, :], MULT)
-
-        banks_c = [psum.tile([P, V], F32, name="c%d" % t, tag="low%d" % t) for t in range(PACK)]
-        quantise_w(2, 0, round_w(2, 0, 40), 1)
-        product_pass(2, 0, banks_c)
-
-        for u in range(2):
-            grouped = keep.tile([P, PACK, P // 2, PACK], BF16, name="last_bf%d" % u, align_bytes=64)
-            by_t = last_raw[u][:].rearrange("p j (m t) -> p m j t", t=4)
-            nc.scalar.copy(grouped[:, 2:4, :, :].rearrange("p t m j -> p m j t"), by_t[:, :, :, 2:4])
-            nc.vector.tensor_copy(grouped[:, 0:2, :, :].rearrange("p t m j -> p m j t"), by_t[:, :, :, 0:2])
-            for t in range(PACK):
-                cols = slice(t * P + u * 64, t * P + (u + 1) * 64)
-                nc.vector.quantize_mx(
-                    out=w_codes[2, 1][:, cols].bitcast(FP8X4),
-                    scales=w_scales[2, 1][:, cols],
-                    in_=grouped[:, t, :, :].rearrange("p m j -> p (m j)"),
-                )
-        product_pass(2, 1, banks_c)
-
-        z_rows = keep.tile([P, PACK, V], BF16, name="z_rows", align_bytes=64)
-        for t in range(PACK - 1):
-            nc.vector.tensor_tensor(z_rows[:, t, :], banks_c[t][:], ab[:, t, :], MULT)
-        t = PACK - 1
+        quantise_w(1, 0, round_w(1, 0, 48), 1)
+        banks_b = open_product(1)
+        quantise_w(1, 1, round_w(1, 1, 80), 2)
+        close_product(1, banks_b)
+        a_sb = keep.tile([P, 2, HALF, PACK], F32, name="a_sb", tag="w_raw11")
         for h in range(2):
-            cols = slice(h * HALF, (h + 1) * HALF)
-            nc.vector.tensor_tensor(z_rows[:, t, cols], banks_c[t][:, cols], ab[:, t, cols], MULT)
-        z_grouped = []
-        for h, copy in enumerate((nc.scalar.copy, nc.vector.tensor_copy)):
-            grouped = keep.tile([P, HALF, PACK], BF16, name="z_bf%d" % h, align_bytes=64)
-            copy(
-                grouped[:].rearrange("p (c i) t -> p c t i", i=4),
-                z_rows[:, :, h * HALF : (h + 1) * HALF].rearrange("p t (c i) -> p c t i", i=4),
+            nc.scalar.copy(a_sb[:, h, :, :], by_triple(banks_a[h]))
+        grouped = round_w(2, 0, 64)
+        ab = [keep.tile([P, HALF, PACK], F32, name="ab%d" % h) for h in range(2)]
+        nc.vector.tensor_tensor(ab[0][:], by_triple(banks_b[0]), a_sb[:, 0, :, :], MULT)
+        quantise_w(2, 0, grouped, 1)
+        banks_c = open_product(2)
+        nc.vector.tensor_tensor(ab[1][:], by_triple(banks_b[1]), a_sb[:, 1, :, :], MULT)
+
+        warm = psum.tile([P, 512], F32, name="warm", tag="sum00")
+        for r in range(2):
+            nc.tensor.matmul_mx(
+                out=warm[:],
+                lhsT=w_codes[2, 0][:, r * P : (r + 1) * P].bitcast(FP8X4),
+                lhsT_scale=w_scales[2, 0][:, r * P : (r + 1) * P],
+                rhs=got_codes[0][:, 0:512].bitcast(FP8X4),
+                rhs_scale=got_scales[:, 0:512],
+                start=True,
+                stop=True,
             )
+        grouped = keep.tile([P, PACK, P, PACK], BF16, name="last_bf", align_bytes=64)
+        by_t = [last_raw[u][:].rearrange("p j (m t) -> p m j t", t=4) for u in range(2)]
+        nc.scalar.copy(grouped[:, :, 0:64, :].rearrange("p t m j -> p m j t"), by_t[0])
+        nc.scalar.copy(grouped[:, :, 64:96, :].rearrange("p t m j -> p m j t"), by_t[1][:, 0:32])
+        nc.vector.tensor_copy(grouped[:, :, 96:128, :].rearrange("p t m j -> p m j t"), by_t[1][:, 32:64])
+        quantise_w(2, 1, grouped, 2)
+        close_product(2, banks_c)
+
+        z_grouped = []
+        for h in range(2):
+            grouped = keep.tile([P, HALF, PACK], BF16, name="z_bf%d" % h, align_bytes=64)
+            nc.vector.tensor_tensor(grouped[:], by_triple(banks_c[h]), ab[h][:], MULT)
             z_grouped.append(grouped)
         for h, copy in enumerate((nc.scalar.copy, nc.vector.tensor_copy)):
             z_codes = keep.tile([P, HALF], U32, name="z_codes%d" % h, align_bytes=64)
@@ -197,7 +208,7 @@ def tile_picked_trilin_none_e_kernel(
                 scales=z_scales[:],
                 in_=z_grouped[h][:].rearrange("p c t -> p (c t)"),
             )
-            acc = psum.tile([P, HALF], F32, name="acc%d" % h, tag="high%d" % h)
+            acc = psum.tile([P, HALF], F32, name="acc%d" % h)
             nc.tensor.matmul_mx(
                 out=acc[:],
                 lhsT=w4_codes[:].bitcast(FP8X4),

@@ -17,9 +17,18 @@ MULT = mybir.AluOpType.mult
 P = 128
 PACK = 4
 K_PASS = P * PACK
-X_COLS = 512
+SCALE_ROWS = 4
 HALF = V // 2
-X_PIECES = {(0, 0): slice(0, 512), (0, 1): slice(512, 1024), (1, 0): slice(0, 512), (1, 1): slice(512, 768), (1, 2): slice(768, 1024)}
+RUN = 4
+
+X_LOADS = (
+    (slice(0, T // 2), slice(T // 2, T)),
+    (slice(0, T // 2), slice(T // 2, 3 * T // 4), slice(3 * T // 4, T)),
+)
+
+SHARE_URGENT = 5 / 8
+SHARE_BUSY = 3 / 8
+SHARE_NONE = 0
 
 
 def tile_picked_trilin_none_e_kernel(
@@ -30,76 +39,64 @@ def tile_picked_trilin_none_e_kernel(
         keep = ctx.enter_context(tc.tile_pool(name="keep", bufs=1))
         psum = ctx.enter_context(tc.psum_pool(name="psum", bufs=1))
 
-        def rows_of(src, g, c0, c1, name):
-            raw = keep.tile([P, PACK, c1 - c0], F32, name=name)
-            rows = src[g * K_PASS : (g + 1) * K_PASS, c0:c1]
-            nc.sync.dma_start(out=raw[:], in_=rows.rearrange("(p j) w -> p j w", j=PACK))
-            return raw
-
         x_scales = keep.tile([P, T], U8, name="x_scales", align_bytes=64)
         nc.gpsimd.memset(x_scales[:], 0)
         w4_plane = keep.tile([P, N], U8, name="w4_plane", align_bytes=64)
         nc.vector.memset(w4_plane[:].bitcast(I32), 0)
-        offsets = keep.tile([P, S // 16], U16, name="offsets")
 
+        def load_pass(src, g, cols, name):
+            raw = keep.tile([P, PACK, cols.stop - cols.start], F32, name=name)
+            rows = src[g * K_PASS : (g + 1) * K_PASS, cols]
+            nc.sync.dma_start(out=raw[:], in_=rows.rearrange("(p j) c -> p j c", j=PACK))
+            return raw
+
+        offsets = keep.tile([P, S // 16], U16, name="offsets")
         x_raw = {}
-        x_raw[0, 0] = rows_of(xT, 0, 0, X_COLS, "x_raw00")
-        nc.sync.dma_start(offsets[:], offs)
-        x_raw[0, 1] = rows_of(xT, 0, X_COLS, T, "x_raw01")
-        for q in range(4):
-            nc.scalar.dma_start(
-                out=w4_plane[32 * q : 32 * q + 4, :].bitcast(I32),
-                in_=w4_scales[0, 4 * q : 4 * q + 4, :].bitcast(I32),
-            )
-        x_raw[1, 0] = rows_of(xT, 1, 0, X_COLS, "x_raw10")
-        x_raw[1, 1] = rows_of(xT, 1, X_COLS, 768, "x_raw11")
-        x_raw[1, 2] = rows_of(xT, 1, 768, T, "x_raw12")
-        w_raw = {}
-        for d, w in enumerate((w1, w2, w3)):
-            for g in range(2):
-                if (d, g) != (2, 1):
-                    w_raw[d, g] = rows_of(w, g, 0, H, "w_raw%d%d" % (d, g))
-        last_raw = [rows_of(w3, 1, u * (H // 2), (u + 1) * (H // 2), "last_raw%d" % u) for u in range(2)]
+        for g, pieces in enumerate(X_LOADS):
+            for u, cols in enumerate(pieces):
+                x_raw[g, u] = load_pass(xT, g, cols, "x_raw%d%d" % (g, u))
+                if (g, u) == (0, 0):
+                    nc.sync.dma_start(offsets[:], offs)
+        whole = slice(0, H)
+        w1_raw = [load_pass(w1, g, whole, "w1_raw%d" % g) for g in range(2)]
+        w2_raw = [load_pass(w2, g, whole, "w2_raw%d" % g) for g in range(2)]
+        w3_raw = load_pass(w3, 0, whole, "w3_raw0")
+        w3_last = [load_pass(w3, 1, slice(u * H // 2, (u + 1) * H // 2), "w3_last%d" % u) for u in range(2)]
         w4_codes = keep.tile([P, N], U32, name="w4_codes", align_bytes=64)
         nc.sync.dma_start(
             out=w4_codes[:].bitcast(I32),
             in_=w4_words[0].rearrange("p n t -> p (n t)").bitcast(I32),
         )
+        for r in range(P // 32):
+            nc.sync.dma_start(
+                out=w4_plane[32 * r : 32 * r + SCALE_ROWS, :].bitcast(I32),
+                in_=w4_scales[0, SCALE_ROWS * r : SCALE_ROWS * (r + 1), :].bitcast(I32),
+            )
+
+        def shared_copy(dst, src, share):
+            count = src.shape[1]
+            cut = int(count * share)
+            nc.scalar.copy(dst[:, cut:], src[:, cut:])
+            if cut:
+                nc.vector.tensor_copy(dst[:, :cut], src[:, :cut])
+
+        def quantise(codes, scales, values):
+            nc.vector.quantize_mx(out=codes.bitcast(FP8X4), scales=scales, in_=values)
 
         x_codes = [keep.tile([P, T], U32, name="x_codes%d" % g, align_bytes=64) for g in range(2)]
         got_codes = [keep.tile([P, S], U32, name="got_codes%d" % g, align_bytes=64) for g in range(2)]
         got_scales = keep.tile([P, S], U8, name="got_scales", align_bytes=64)
-
-        def round_x(g, u, on_vector):
-            raw = x_raw[g, u]
-            width = raw.shape[2]
-            grouped = keep.tile([P, width, PACK], BF16, name="x_bf%d%d" % (g, u), align_bytes=64)
-            for copy, c0, c1 in ((nc.scalar.copy, on_vector, width), (nc.vector.tensor_copy, 0, on_vector)):
-                if c1 > c0:
-                    copy(
-                        grouped[:, c0:c1, :].rearrange("p (c i) j -> p c j i", i=4),
-                        raw[:, :, c0:c1].rearrange("p j (c i) -> p c j i", i=4),
-                    )
-            return grouped
-
-        def quantise_x(g, u, grouped):
-            cols = X_PIECES[g, u]
-            nc.vector.quantize_mx(
-                out=x_codes[g][:, cols].bitcast(FP8X4),
-                scales=x_scales[4 * g : P, cols],
-                in_=grouped[:].rearrange("p c j -> p (c j)"),
-            )
-
-        def round_w(d, g, on_vector):
-            raw = w_raw[d, g]
-            grouped = keep.tile([P, PACK, P, PACK], BF16, name="w_bf%d%d" % (d, g), align_bytes=64)
-            for copy, m0, m1 in ((nc.scalar.copy, on_vector, P), (nc.vector.tensor_copy, 0, on_vector)):
-                if m1 > m0:
-                    copy(
-                        grouped[:, :, m0:m1, :].rearrange("p t m j -> p m j t"),
-                        raw[:, :, 4 * m0 : 4 * m1].rearrange("p j (m t) -> p m j t", t=4),
-                    )
-            return grouped
+        for g, pieces in enumerate(X_LOADS):
+            for u, cols in enumerate(pieces):
+                x_bf = keep.tile([P, cols.stop - cols.start, PACK], BF16, name="x_bf%d%d" % (g, u), align_bytes=64)
+                shared_copy(
+                    x_bf[:].rearrange("p (c i) j -> p c j i", i=RUN),
+                    x_raw[g, u][:].rearrange("p j (c i) -> p c j i", i=RUN),
+                    SHARE_URGENT if g == 0 else SHARE_BUSY,
+                )
+                quantise(x_codes[g][:, cols], x_scales[SCALE_ROWS * g : P, cols], x_bf[:].rearrange("p c j -> p (c j)"))
+            nc.vector.tensor_copy(got_codes[g][:], x_codes[g][:].indirect(offsets[:]))
+        nc.vector.tensor_copy(got_scales[:], x_scales[:].indirect(offsets[:]))
 
         w_codes = {}
         w_scales = {}
@@ -108,16 +105,28 @@ def tile_picked_trilin_none_e_kernel(
                 w_codes[d, g] = keep.tile([P, H], U32, name="w_codes%d%d" % (d, g), align_bytes=64)
                 w_scales[d, g] = keep.tile([P, H], U8, name="w_scales%d%d" % (d, g), align_bytes=64)
 
-        def quantise_w(d, g, grouped, calls):
-            flat = grouped[:].rearrange("p t m j -> p (t m j)")
+        def dealt_tile(d, g):
+            return keep.tile([P, PACK, P, PACK], BF16, name="w_bf%d%d" % (d, g), align_bytes=64)
+
+        def deal(w_bf, raw, share):
+            shared_copy(
+                w_bf.rearrange("p t m j -> p m j t"),
+                raw[:].rearrange("p j (m t) -> p m j t", t=PACK),
+                share,
+            )
+
+        def quantise_w(d, g, w_bf, calls):
+            flat = w_bf[:].rearrange("p t m j -> p (t m j)")
             width = H // calls
             for c in range(calls):
                 cols = slice(c * width, (c + 1) * width)
-                nc.vector.quantize_mx(
-                    out=w_codes[d, g][:, cols].bitcast(FP8X4),
-                    scales=w_scales[d, g][:, cols],
-                    in_=flat[:, PACK * c * width : PACK * (c + 1) * width],
-                )
+                values = flat[:, PACK * cols.start : PACK * cols.stop]
+                quantise(w_codes[d, g][:, cols], w_scales[d, g][:, cols], values)
+
+        def prepare_w(d, g, raw, share, calls):
+            w_bf = dealt_tile(d, g)
+            deal(w_bf[:], raw, share)
+            quantise_w(d, g, w_bf, calls)
 
         def one_pass(d, g, t, h, bank):
             cols = slice(t * P, (t + 1) * P)
@@ -127,87 +136,73 @@ def tile_picked_trilin_none_e_kernel(
                 lhsT=w_codes[d, g][:, cols].bitcast(FP8X4),
                 lhsT_scale=w_scales[d, g][:, cols],
                 rhs=got_codes[g][:, picked].bitcast(FP8X4),
-                rhs_scale=got_scales[4 * g : P, picked],
+                rhs_scale=got_scales[SCALE_ROWS * g : P, picked],
                 start=(g == 0),
                 stop=(g == 1),
             )
 
+        def open_bank(d, h, tag):
+            bank = psum.tile([P, PACK, HALF], F32, name="sums%d%d" % (d, h), tag=tag)
+            one_pass(d, 0, 0, h, bank)
+            return bank
+
+        def close_bank(d, h, bank):
+            one_pass(d, 1, 0, h, bank)
+            for t in range(1, PACK):
+                one_pass(d, 0, t, h, bank)
+                one_pass(d, 1, t, h, bank)
+
         def open_product(d):
-            banks = [psum.tile([P, PACK, HALF], F32, name="sum%d%d" % (d, h)) for h in range(2)]
-            for h in range(2):
-                one_pass(d, 0, 0, h, banks[h])
-            return banks
+            return [open_bank(d, h, "sums%d%d" % (d, h)) for h in range(2)]
 
         def close_product(d, banks):
             for h in range(2):
-                one_pass(d, 1, 0, h, banks[h])
-                for t in range(1, PACK):
-                    one_pass(d, 0, t, h, banks[h])
-                    one_pass(d, 1, t, h, banks[h])
+                close_bank(d, h, banks[h])
 
         def by_triple(bank):
             return bank[:].rearrange("p t v -> p v t")
 
-        quantise_x(0, 0, round_x(0, 0, 384))
-        quantise_x(0, 1, round_x(0, 1, 320))
-        nc.vector.tensor_copy(got_codes[0][:], x_codes[0][:].indirect(offsets[:]))
-        quantise_x(1, 0, round_x(1, 0, 128))
-        quantise_x(1, 1, round_x(1, 1, 160))
-        quantise_x(1, 2, round_x(1, 2, 64))
-        nc.vector.tensor_copy(got_codes[1][:], x_codes[1][:].indirect(offsets[:]))
-        nc.vector.tensor_copy(got_scales[:], x_scales[:].indirect(offsets[:]))
+        prepare_w(0, 0, w1_raw[0], SHARE_NONE, 1)
+        first = open_product(0)
+        prepare_w(0, 1, w1_raw[1], SHARE_BUSY, 1)
+        close_product(0, first)
 
-        quantise_w(0, 0, round_w(0, 0, 0), 1)
-        banks_a = open_product(0)
-        quantise_w(0, 1, round_w(0, 1, 48), 1)
-        close_product(0, banks_a)
+        prepare_w(1, 0, w2_raw[0], SHARE_BUSY, 1)
+        second = [open_bank(1, 0, "second")]
+        prepare_w(1, 1, w2_raw[1], SHARE_URGENT, 2)
+        close_bank(1, 0, second[0])
 
-        quantise_w(1, 0, round_w(1, 0, 48), 1)
-        banks_b = open_product(1)
-        quantise_w(1, 1, round_w(1, 1, 80), 2)
-        close_product(1, banks_b)
-        a_sb = keep.tile([P, 2, HALF, PACK], F32, name="a_sb", tag="w_raw11")
+        first_sb = keep.tile([P, 2, HALF, PACK], F32, name="first_sb", tag="w2_raw1")
         for h in range(2):
-            nc.scalar.copy(a_sb[:, h, :, :], by_triple(banks_a[h]))
-        grouped = round_w(2, 0, 64)
-        ab = [keep.tile([P, HALF, PACK], F32, name="ab%d" % h) for h in range(2)]
-        nc.vector.tensor_tensor(ab[0][:], by_triple(banks_b[0]), a_sb[:, 0, :, :], MULT)
-        quantise_w(2, 0, grouped, 1)
-        banks_c = open_product(2)
-        nc.vector.tensor_tensor(ab[1][:], by_triple(banks_b[1]), a_sb[:, 1, :, :], MULT)
+            nc.scalar.copy(first_sb[:, h, :, :], by_triple(first[h]))
 
-        warm = psum.tile([P, 512], F32, name="warm", tag="sum00")
-        for r in range(2):
-            nc.tensor.matmul_mx(
-                out=warm[:],
-                lhsT=w_codes[2, 0][:, r * P : (r + 1) * P].bitcast(FP8X4),
-                lhsT_scale=w_scales[2, 0][:, r * P : (r + 1) * P],
-                rhs=got_codes[0][:, 0:512].bitcast(FP8X4),
-                rhs_scale=got_scales[:, 0:512],
-                start=True,
-                stop=True,
-            )
-        grouped = keep.tile([P, PACK, P, PACK], BF16, name="last_bf", align_bytes=64)
-        by_t = [last_raw[u][:].rearrange("p j (m t) -> p m j t", t=4) for u in range(2)]
-        nc.scalar.copy(grouped[:, :, 0:64, :].rearrange("p t m j -> p m j t"), by_t[0])
-        nc.scalar.copy(grouped[:, :, 64:96, :].rearrange("p t m j -> p m j t"), by_t[1][:, 0:32])
-        nc.vector.tensor_copy(grouped[:, :, 96:128, :].rearrange("p t m j -> p m j t"), by_t[1][:, 32:64])
-        quantise_w(2, 1, grouped, 2)
-        close_product(2, banks_c)
+        w_bf = dealt_tile(2, 0)
+        deal(w_bf[:], w3_raw, SHARE_URGENT)
+        two = [keep.tile([P, HALF, PACK], F32, name="two0")]
+        nc.vector.tensor_tensor(two[0][:], by_triple(second[0]), first_sb[:, 0, :, :], MULT)
+        quantise_w(2, 0, w_bf, 1)
 
-        z_grouped = []
+        second.append(open_bank(1, 1, "second"))
+        close_bank(1, 1, second[1])
+        third = open_product(2)
+
+        w_bf = dealt_tile(2, 1)
+        deal(w_bf[:, :, : P // 2, :], w3_last[0], SHARE_NONE)
+        deal(w_bf[:, :, P // 2 :, :], w3_last[1], SHARE_URGENT)
+        quantise_w(2, 1, w_bf, 2)
+        close_product(2, third)
+
+        two.append(keep.tile([P, HALF, PACK], F32, name="two1", tag="w3_last1"))
+        nc.vector.tensor_tensor(two[1][:], by_triple(second[1]), first_sb[:, 1, :, :], MULT)
+
+        z_bf = [keep.tile([P, HALF, PACK], BF16, name="z_bf%d" % h, align_bytes=64) for h in range(2)]
         for h in range(2):
-            grouped = keep.tile([P, HALF, PACK], BF16, name="z_bf%d" % h, align_bytes=64)
-            nc.vector.tensor_tensor(grouped[:], by_triple(banks_c[h]), ab[h][:], MULT)
-            z_grouped.append(grouped)
-        for h, copy in enumerate((nc.scalar.copy, nc.vector.tensor_copy)):
+            nc.vector.tensor_tensor(z_bf[h][:], by_triple(third[h]), two[h][:], MULT)
+
+        for h, copy_out in enumerate((nc.scalar.copy, nc.vector.tensor_copy)):
             z_codes = keep.tile([P, HALF], U32, name="z_codes%d" % h, align_bytes=64)
             z_scales = keep.tile([P, HALF], U8, name="z_scales%d" % h, align_bytes=64)
-            nc.vector.quantize_mx(
-                out=z_codes[:].bitcast(FP8X4),
-                scales=z_scales[:],
-                in_=z_grouped[h][:].rearrange("p c t -> p (c t)"),
-            )
+            quantise(z_codes[:], z_scales[:], z_bf[h][:].rearrange("p v t -> p (v t)"))
             acc = psum.tile([P, HALF], F32, name="acc%d" % h)
             nc.tensor.matmul_mx(
                 out=acc[:],
@@ -219,5 +214,5 @@ def tile_picked_trilin_none_e_kernel(
                 stop=True,
             )
             result = keep.tile([P, HALF], F32, name="result%d" % h)
-            copy(result[:], acc[:])
+            copy_out(result[:], acc[:])
             nc.sync.dma_start(out=out[:, h * HALF : (h + 1) * HALF], in_=result[:])

from contextlib import ExitStack

import concourse.mybir as mybir

K, T, S, V, H, N = 1024, 1024, 768, 256, 512, 128
FLOPS = 3 * 2 * K * H * V + 2 * H * N * V

F32 = mybir.dt.float32
BF16 = mybir.dt.bfloat16
I32 = mybir.dt.int32
U32 = mybir.dt.uint32
U16 = mybir.dt.uint16
U8 = mybir.dt.uint8
FP8X4 = mybir.dt.float8_e4m3fn_x4
MULT = mybir.AluOpType.mult

P = 128
PACK = 4
K_PASS = P * PACK
SCALE_ROWS = 4
HALF = V // 2
RUN = 4

X_LOADS = (
    (slice(0, T // 2), slice(T // 2, T)),
    (slice(0, T // 2), slice(T // 2, 3 * T // 4), slice(3 * T // 4, T)),
)

SHARE_URGENT = 5 / 8
SHARE_BUSY = 3 / 8
SHARE_NONE = 0


def tile_picked_trilin_none_e_kernel(
    tc, xT, w1, w2, w3, w4_words, w4_scales, offs, out
):
    nc = tc.nc
    with ExitStack() as ctx:
        keep = ctx.enter_context(tc.tile_pool(name="keep", bufs=1))
        psum = ctx.enter_context(tc.psum_pool(name="psum", bufs=1))

        x_scales = keep.tile([P, T], U8, name="x_scales", align_bytes=64)
        nc.gpsimd.memset(x_scales[:], 0)
        w4_plane = keep.tile([P, N], U8, name="w4_plane", align_bytes=64)
        nc.vector.memset(w4_plane[:].bitcast(I32), 0)

        def load_pass(src, g, cols, name):
            raw = keep.tile([P, PACK, cols.stop - cols.start], F32, name=name)
            rows = src[g * K_PASS : (g + 1) * K_PASS, cols]
            nc.sync.dma_start(out=raw[:], in_=rows.rearrange("(p j) c -> p j c", j=PACK))
            return raw

        offsets = keep.tile([P, S // 16], U16, name="offsets")
        x_raw = {}
        for g, pieces in enumerate(X_LOADS):
            for u, cols in enumerate(pieces):
                x_raw[g, u] = load_pass(xT, g, cols, "x_raw%d%d" % (g, u))
                if (g, u) == (0, 0):
                    nc.sync.dma_start(offsets[:], offs)
        whole = slice(0, H)
        w1_raw = [load_pass(w1, g, whole, "w1_raw%d" % g) for g in range(2)]
        w2_raw = [load_pass(w2, g, whole, "w2_raw%d" % g) for g in range(2)]
        w3_raw = load_pass(w3, 0, whole, "w3_raw0")
        w3_last = [load_pass(w3, 1, slice(u * H // 2, (u + 1) * H // 2), "w3_last%d" % u) for u in range(2)]
        w4_codes = keep.tile([P, N], U32, name="w4_codes", align_bytes=64)
        nc.sync.dma_start(
            out=w4_codes[:].bitcast(I32),
            in_=w4_words[0].rearrange("p n t -> p (n t)").bitcast(I32),
        )
        for r in range(P // 32):
            nc.sync.dma_start(
                out=w4_plane[32 * r : 32 * r + SCALE_ROWS, :].bitcast(I32),
                in_=w4_scales[0, SCALE_ROWS * r : SCALE_ROWS * (r + 1), :].bitcast(I32),
            )

        def shared_copy(dst, src, share):
            count = src.shape[1]
            cut = int(count * share)
            nc.scalar.copy(dst[:, cut:], src[:, cut:])
            if cut:
                nc.vector.tensor_copy(dst[:, :cut], src[:, :cut])

        def quantise(codes, scales, values):
            nc.vector.quantize_mx(out=codes.bitcast(FP8X4), scales=scales, in_=values)

        x_codes = [keep.tile([P, T], U32, name="x_codes%d" % g, align_bytes=64) for g in range(2)]
        got_codes = [keep.tile([P, S], U32, name="got_codes%d" % g, align_bytes=64) for g in range(2)]
        got_scales = keep.tile([P, S], U8, name="got_scales", align_bytes=64)
        for g, pieces in enumerate(X_LOADS):
            for u, cols in enumerate(pieces):
                x_bf = keep.tile([P, cols.stop - cols.start, PACK], BF16, name="x_bf%d%d" % (g, u), align_bytes=64)
                shared_copy(
                    x_bf[:].rearrange("p (c i) j -> p c j i", i=RUN),
                    x_raw[g, u][:].rearrange("p j (c i) -> p c j i", i=RUN),
                    SHARE_URGENT if g == 0 else SHARE_BUSY,
                )
                quantise(x_codes[g][:, cols], x_scales[SCALE_ROWS * g : P, cols], x_bf[:].rearrange("p c j -> p (c j)"))
            nc.vector.tensor_copy(got_codes[g][:], x_codes[g][:].indirect(offsets[:]))
        nc.vector.tensor_copy(got_scales[:], x_scales[:].indirect(offsets[:]))

        w_codes = {}
        w_scales = {}
        for d in range(3):
            for g in range(2):
                w_codes[d, g] = keep.tile([P, H], U32, name="w_codes%d%d" % (d, g), align_bytes=64)
                w_scales[d, g] = keep.tile([P, H], U8, name="w_scales%d%d" % (d, g), align_bytes=64)

        def dealt_tile(d, g):
            return keep.tile([P, PACK, P, PACK], BF16, name="w_bf%d%d" % (d, g), align_bytes=64)

        def deal(w_bf, raw, share):
            shared_copy(
                w_bf.rearrange("p t m j -> p m j t"),
                raw[:].rearrange("p j (m t) -> p m j t", t=PACK),
                share,
            )

        def quantise_w(d, g, w_bf, calls):
            flat = w_bf[:].rearrange("p t m j -> p (t m j)")
            width = H // calls
            for c in range(calls):
                cols = slice(c * width, (c + 1) * width)
                values = flat[:, PACK * cols.start : PACK * cols.stop]
                quantise(w_codes[d, g][:, cols], w_scales[d, g][:, cols], values)

        def prepare_w(d, g, raw, share, calls):
            w_bf = dealt_tile(d, g)
            deal(w_bf[:], raw, share)
            quantise_w(d, g, w_bf, calls)

        def one_pass(d, g, t, h, bank):
            cols = slice(t * P, (t + 1) * P)
            picked = slice(d * V + h * HALF, d * V + (h + 1) * HALF)
            nc.tensor.matmul_mx(
                out=bank[:, t, :],
                lhsT=w_codes[d, g][:, cols].bitcast(FP8X4),
                lhsT_scale=w_scales[d, g][:, cols],
                rhs=got_codes[g][:, picked].bitcast(FP8X4),
                rhs_scale=got_scales[SCALE_ROWS * g : P, picked],
                start=(g == 0),
                stop=(g == 1),
            )

        def open_bank(d, h, tag):
            bank = psum.tile([P, PACK, HALF], F32, name="sums%d%d" % (d, h), tag=tag)
            one_pass(d, 0, 0, h, bank)
            return bank

        def close_bank(d, h, bank):
            one_pass(d, 1, 0, h, bank)
            for t in range(1, PACK):
                one_pass(d, 0, t, h, bank)
                one_pass(d, 1, t, h, bank)

        def open_product(d):
            return [open_bank(d, h, "sums%d%d" % (d, h)) for h in range(2)]

        def close_product(d, banks):
            for h in range(2):
                close_bank(d, h, banks[h])

        def by_triple(bank):
            return bank[:].rearrange("p t v -> p v t")

        prepare_w(0, 0, w1_raw[0], SHARE_NONE, 1)
        first = open_product(0)
        prepare_w(0, 1, w1_raw[1], SHARE_BUSY, 1)
        close_product(0, first)

        prepare_w(1, 0, w2_raw[0], SHARE_BUSY, 1)
        second = [open_bank(1, 0, "second")]
        prepare_w(1, 1, w2_raw[1], SHARE_URGENT, 2)
        close_bank(1, 0, second[0])

        first_sb = keep.tile([P, 2, HALF, PACK], F32, name="first_sb", tag="w2_raw1")
        for h in range(2):
            nc.scalar.copy(first_sb[:, h, :, :], by_triple(first[h]))

        w_bf = dealt_tile(2, 0)
        deal(w_bf[:], w3_raw, SHARE_URGENT)
        two = [keep.tile([P, HALF, PACK], F32, name="two0")]
        nc.vector.tensor_tensor(two[0][:], by_triple(second[0]), first_sb[:, 0, :, :], MULT)
        quantise_w(2, 0, w_bf, 1)

        second.append(open_bank(1, 1, "second"))
        close_bank(1, 1, second[1])
        third = open_product(2)

        w_bf = dealt_tile(2, 1)
        deal(w_bf[:, :, : P // 2, :], w3_last[0], SHARE_NONE)
        deal(w_bf[:, :, P // 2 :, :], w3_last[1], SHARE_URGENT)
        quantise_w(2, 1, w_bf, 2)
        close_product(2, third)

        two.append(keep.tile([P, HALF, PACK], F32, name="two1", tag="w3_last1"))
        nc.vector.tensor_tensor(two[1][:], by_triple(second[1]), first_sb[:, 1, :, :], MULT)

        z_bf = [keep.tile([P, HALF, PACK], BF16, name="z_bf%d" % h, align_bytes=64) for h in range(2)]
        for h in range(2):
            nc.vector.tensor_tensor(z_bf[h][:], by_triple(third[h]), two[h][:], MULT)

        for h, copy_out in enumerate((nc.scalar.copy, nc.vector.tensor_copy)):
            z_codes = keep.tile([P, HALF], U32, name="z_codes%d" % h, align_bytes=64)
            z_scales = keep.tile([P, HALF], U8, name="z_scales%d" % h, align_bytes=64)
            quantise(z_codes[:], z_scales[:], z_bf[h][:].rearrange("p v t -> p (v t)"))
            acc = psum.tile([P, HALF], F32, name="acc%d" % h)
            nc.tensor.matmul_mx(
                out=acc[:],
                lhsT=w4_codes[:].bitcast(FP8X4),
                lhsT_scale=w4_plane[:],
                rhs=z_codes[:].bitcast(FP8X4),
                rhs_scale=z_scales[:],
                start=True,
                stop=True,
            )
            result = keep.tile([P, HALF], F32, name="result%d" % h)
            copy_out(result[:], acc[:])
            nc.sync.dma_start(out=out[:, h * HALF : (h + 1) * HALF], in_=result[:])
